import numpy as np, ml_dtypes
CORES = [9,25,41,57]
N = 4
import mx_ref
BF = ml_dtypes.bfloat16
def gentries(a):
    return np.ascontiguousarray(a.reshape(8, 16, -1).transpose(0, 2, 1)).reshape(8, -1)
def gtable(e):
    e = np.asarray(e); return np.ascontiguousarray(e.reshape(8, -1, 16).transpose(0, 2, 1)).reshape(128, -1).astype(np.int32)
def gcols(t, e):
    v = np.concatenate([t.reshape(8, 16, -1, 4), np.zeros((8, 16, 1, 4), BF)], axis=2)
    return np.ascontiguousarray(np.stack([v[g][:, e[g]] for g in range(8)])).reshape(128, -1)
def tile(rs):
    return np.stack(rs, axis=2).reshape(128, -1).astype(BF)
def cut(t, i, w=512):
    return t[:, w * i:w * i + w]
def pick(q, e):
    c = np.concatenate([q[0].reshape(128, -1, 4), np.zeros((128, 1, 4), np.uint8)], axis=1); s = np.concatenate([q[1], np.ones((16, 1), np.uint8)], axis=1)
    return (np.ascontiguousarray(c[:, e].reshape(128, -1)), np.ascontiguousarray(s[:, e]))
def join(*qs):
    return (np.concatenate([q[0] for q in qs], axis=1), np.concatenate([q[1] for q in qs], axis=1))
def put(q, e, v):
    c, s = q[0].reshape(128, -1, 4).copy(), q[1].copy(); c[:, e] = v[0].reshape(128, -1, 4); s[:, e] = v[1]
    return (c.reshape(128, -1), s)
def pk(c, s):
    return (np.ascontiguousarray(c), mx_ref.live(s))
def emit(q):
    return q[0], q[1]
def packed(v, rng):
    q = [mx_ref.quantize(np.ascontiguousarray(v[r])) for r in range(N)]
    return np.stack([a for a, b in q]), np.stack([mx_ref.plane(b, rng) for a, b in q])
def values_of_codes():
    e, c = np.zeros((128, 128, 4), np.float32), np.zeros((128, 2, 4), np.uint8)
    e[np.arange(128), np.arange(128), 0] = 1
    c[:127, :, 0] = np.arange(256).reshape(2, 128).T[:127]
    return mx_ref.matmul(mx_ref.quantize(e.reshape(128, 512).astype(BF)), (c.reshape(128, 8), np.full((16, 2), 127, np.uint8))).T.reshape(-1).astype(np.float64)
CODE_VALUE, SCALE_VALUE = values_of_codes(), 2.0 ** (np.arange(256) - 127.0)
def decode(q):
    return (CODE_VALUE[q[0]].reshape(16, 8, -1, 4) * SCALE_VALUE[q[1]][:, None, :, None] + 0.0).reshape(128, -1).astype(np.float32)
def f(rng, *shape):
    return mx_ref.flush((rng.standard_normal(shape, dtype=np.float32) * np.exp2(rng.integers(-2, 3, shape[:-1] + (1,)))).astype(BF))
def wide(rng, *shape, cols=0):
    v = rng.standard_normal(shape, dtype=np.float32) * np.exp2(rng.integers(-12, 13, shape)).astype(np.float32)
    if cols: v *= np.repeat(np.exp2(rng.integers(-cols, cols + 1, shape[:-2] + (1, shape[-1] // 4))) * (rng.random(shape[:-2] + (1, shape[-1] // 4)) > 0.0625), 4, axis=-1).astype(np.float32)
    return mx_ref.flush(v.astype(BF))
C, K, R = 224, 64, 3
def order(p):
    return np.argsort(-(p[::16] + np.float32(0.0)), axis=1, kind="stable")
def larger(a, b):
    return np.maximum(a.astype(np.float32), b.astype(np.float32)).astype(BF)
def numbers_of(rng):
    return {"x": np.array(f(rng, N, 128, 4 * C)), "u": np.array(f(rng, N, 128, 512)), "v": np.array(f(rng, N, 128, 512))}
def weights(rng, still=[]):
    w = np.array(f(rng, N, 128, 2048)).reshape(N, 8, 16, 4, 8, 16, 4)
    for i in still:
        w[:, :, i] = 0
        w[:, :, :, :, :, i] = 0
    c, p = packed(w.reshape(N, 128, 2048), rng)
    return {"wc": c, "ws": p}
def lists_of(rng):
    return np.stack([gtable(rng.integers(0, C, (8, R * C))) for r in range(N)])
def signs(rng):
    return np.stack([rng.permutation(8) % 2 * 2.0 - 1.0 for r in range(N)])
def setup_inputs(rng):
    return {**numbers_of(rng), **weights(rng), "nb": lists_of(rng)}
def setup_inputs_ties(rng):
    d = numbers_of(rng)
    e = rng.permutation(N)
    x = d["x"].reshape(N, 8, 16, C, 4)
    for r in range(N):
        k = np.zeros(C, int) if r == e[0] else rng.permutation(C) % 3
        a = x[r][:, :8, :3].copy()
        a[:, :, 2] = 0
        x[r][:, :8] = a[:, :, k]
    x[e[1]][:, :8] = 0
    u = d["u"].reshape(N, 8, 16, 8, 16, 4)
    k = u.copy()
    u[:, :, :, :, :3] = 0
    for g in range(8): u[:, g, :8, g, :3] = k[:, g, :8, g, :3]
    return {"x": x.reshape(N, 128, 4 * C), "u": u.reshape(N, 128, 512), "v": d["v"], **weights(rng, range(8)), "nb": lists_of(rng)}
def setup_inputs_near(rng):
    d = numbers_of(rng)
    x = d["x"].astype(np.float32).reshape(N, 8, 16, C, 4)
    u = d["u"].reshape(N, 128, 128, 4)
    x[:, :, 0] = 0
    x[:, :, 10] = 0
    for i in range(3): u[:, :, i::16] = 0
    c = rng.permutation(8) % 2 * 2.0 - 1.0
    first = int(rng.integers(N))
    upper = np.arange(C) // (C // 2)
    for n in range(N):
        r = (first + n) % N
        i = (np.arange(C) + rng.integers(0, C, (8, 1))) % (C // 2) * 2 + upper
        one = n < N // 2
        s = i // 2 if one else i
        size = 1.0 if one else 2.0 ** -7
        k = 1.0 if one and n % 2 == 0 else 2.0 ** -30
        if one:
            x[r, :, 0, :, 0] = c[:, None]
            for g in rng.permutation(8)[:4]: x[r, g, 0, rng.integers(C), 0] *= np.float32(2.0 ** 30)
        z = ((s[:, :, None] >> np.arange(8)) & 1) * np.exp2(np.arange(8) - 23.0) * size
        x[r, :, 8] = z[:, :, :4]
        x[r, :, 9] = z[:, :, 4:]
        x[r, :, 10, :, 0] = rng.integers(-1, 2, (8, C)) * 2.0 ** -23 * size
        x[r, :, 11:] = rng.integers(4, 8, (8, 5, C, 4)) * rng.choice([-1.0, 1.0], (8, 5, C, 4)) * 2.0 ** -20 * size
        for h in range(0, 128, 16):
            u[r, h, h:h + 2, 0] = k
            u[r, h + 8:h + 10, h] = k
            u[r, h + 8:h + 10, h + 1] = (k * rng.choice([-1.0, 1.0], (2, 4))).astype(np.float32).astype(BF)
            u[r, h + 10, h + 2, 0] = k
    return {"x": x.reshape(N, 128, 4 * C).astype(BF), "u": u.reshape(N, 128, 512), "v": d["v"], **weights(rng, [0, 8, 9, 10, 11, 12, 13, 14, 15]), "nb": lists_of(rng)}
def setup_inputs_huge(rng):
    d = numbers_of(rng)
    c = np.stack([rng.permutation(C) % 2 * 2.0 - 1.0 for r in range(N)])
    low = (int(rng.integers(N)) + np.arange(N // 2)) % N
    c[low] = -1
    size = np.where(c < 0, -2.0 ** 30, 2.0 ** 28)
    size[low, C - K:] *= 0.7
    x = (0.6 + 0.2 * rng.random((N, 128, C, 4))) * size[:, None, :, None]
    u = d["u"].reshape(N, 128, 128, 4)
    for i in range(3):
        a = 2.0 ** 30 * (1 - 0.25 * rng.random((N, 128, 8, 4))) * signs(rng)[:, None, :, None]
        u[:, :, i::16] = a.astype(np.float32).astype(BF)
    w = np.zeros((N, 128, 4, 128, 4), np.float32)
    i = np.arange(128)
    for b in range(4): w[:, i, b, i, b] = 16 - 32 * (i % 2)
    wc, ws = packed(w.reshape(N, 128, 2048).astype(BF), rng)
    return {"x": x.astype(np.float32).reshape(N, 128, 4 * C).astype(BF), "u": u.reshape(N, 128, 512), "v": d["v"], "wc": wc, "ws": ws, "nb": lists_of(rng)}
def setup_inputs_chains(rng):
    d = numbers_of(rng)
    x = d["x"].astype(np.float32).reshape(N, 8, 16, C, 4)
    u = d["u"].reshape(N, 128, 128, 4)
    h, e, k = rng.permutation(8).tolist(), rng.permutation(N), np.arange(N)[:, None]
    x[:, :, :3] = 0
    x[:, :, 0, :, 0] = rng.integers(1, 8, (N, 8, C))
    x[:, h[0], 0, :, 0] = 1 + k
    x[:, h[1], 0, :, 0] = N - k
    x[:, :, 1, :, 0] = rng.integers(1, 16, (N, 8, C))
    x[:, :, 2, :, 0] = rng.integers(-1, 2, (N, 8, C))
    x[e[0], :, 2, :, 0] = 0
    x[e[1], :, 2, :, 0] = -1
    for i in range(3): u[:, :, i::16] = 0
    for g in range(8):
        i = 16 * g
        u[:, i + (0 if g in h[2:6] else 1), i, 0] = -1 if g in h[4:6] else 1
        u[:, i, i + 1, 0] = 1
        u[:, i + 2, i + 2, 0] = 1
    nb = rng.integers(0, C, (N, 8, R, C))
    for r in range(N):
        q = rng.permutation(8)
        nb[r, q[0]] = rng.integers(0, C)
        nb[r, q[1]] = np.arange(C)
        nb[r, q[2]] = C - 1 - np.arange(C)
        nb[r, q[3]] = (np.arange(C) + 1) % C
    nb = np.stack([gtable(nb[r].reshape(8, R * C)) for r in range(N)])
    return {"x": x.reshape(N, 128, 4 * C).astype(BF), "u": u.reshape(N, 128, 512), "v": d["v"], **weights(rng, [0, 1, 2]), "nb": nb}
def setup_inputs_spread(rng):
    d = setup_inputs(rng)
    d["x"] = wide(rng, N, 128, 4 * C, cols=6)
    return d
def check_inputs(d):
    b = []
    for k in ("x", "u", "v"):
        a = np.abs(d[k].astype(np.float32))
        if not (np.isfinite(a).all() and ((a == 0) | (a >= 2.0 ** -30) & (a <= 2.0 ** 30)).all()): b.append("a value of " + k)
    if ((d["wc"] & 0x7F) == 0x7F).any(): b.append("a code of wc that is no number")
    none, least, most = [emit(mx_ref.quantize(np.full((128, 16), k, np.float32).astype(BF)))[1][0, 0] for k in (0.0, 2.0 ** -30, 2.0 ** 30)]
    for r in range(N):
        s = mx_ref.live(d["ws"][r])
        if ((s != none) & ((s < least) | (s > most))).any(): b.append("a scale of ws")
    if (d["nb"] < 0).any() or (d["nb"] >= C).any(): b.append("an entry of nb")
    return b
def reference(x, u, v, wc, ws, nb):
    qu = [mx_ref.quantize(u[r]) for r in range(N)]
    lay = [pk(wc[r], ws[r]) for r in range(N)]
    now = [x[r] for r in range(N)]
    far = [gentries(nb[r]).reshape(8, R, C) for r in range(N)]
    guests = [np.zeros((128, 0), BF) for r in range(N)]
    place = np.arange(C)
    p = np.zeros((N, 8, C), np.int64) + place
    for t in range(R):
        sent = []
        for r in range(N):
            s = mx_ref.matmul(qu[r], mx_ref.quantize(now[r]))
            p[r] = np.where(s[2::16] < 0, place, p[r])
            sent.append(mx_ref.quantize(gcols(now[r], order(s)[:, :K])))
        came = decode(join(*sent)).astype(BF)
        for r in range(N):
            guests[r] = np.concatenate([guests[r], cut(came, (r - 1) % N, 4 * K)], axis=1)
            pool = np.concatenate([now[r], guests[r]], axis=1)
            cand = np.stack([p[r], np.take_along_axis(p[r], far[r][:, t], axis=1), np.zeros((8, C), np.int64) + C + K * t + place % K])
            met = [larger(now[r], gcols(pool, cand[k])) for k in range(3)]
            best = np.argmax(np.stack([mx_ref.matmul(qu[r], mx_ref.quantize(met[k]))[1::16] + np.float32(0.0) for k in range(3)]), axis=0)
            p[r] = np.take_along_axis(cand, best[None], axis=0)[0]
            q = mx_ref.quantize(gcols(np.concatenate(met, axis=1), best * C + place))
            now[r] = tile([np.maximum(mx_ref.matmul(pick(lay[r], np.arange(128 * b, 128 * b + 128)), q), np.float32(0.0)) * np.float32(0.015625) + now[r][:, b::4].astype(np.float32) for b in range(4)])
    y, op = np.zeros((N, 128, C), np.float32), np.zeros((N, 8, C), np.float32)
    oc, osc = np.zeros((N, 128, 4 * C), np.uint8), np.zeros((N, 16, C), np.uint8)
    for r in range(N):
        q = mx_ref.quantize(now[r])
        y[r] = mx_ref.matmul(mx_ref.quantize(v[r]), q)
        op[r] = p[r]
        oc[r], osc[r] = emit(q)
    return {"y": y, "op": op, "oc": oc, "osc": osc}

@@ -1,0 +1,376 @@
+from concourse.mybir import dt, AluOpType, ActivationFunctionType
+
+C, K, R = 224, 64, 3
+CV = [5, 6, 7, 8, 9]
+CA = [c for c in range(14) if c not in CV]
+Q4, U8, BF, F32, I32, U16 = "float8_e4m3fn_x4", "uint8", "bfloat16", "float32", "int32", "uint16"
+
+
+def _sb(n, d):
+    return ("sbuf", [128, n], d)
+
+
+SCRATCH = {
+    "xs": _sb(4 * C, BF), "pool": _sb(4 * C + 2 * 4 * K, BF), "jw": _sb(3072, BF), "zt": _sb(4 * C, BF), "dd": _sb(4 * C, BF),
+    "ut": _sb(512, BF), "vt": _sb(512, BF), "et": _sb(2048, BF),
+    "qu": _sb(128, Q4), "su": _sb(128, U8), "qu3": _sb(384, Q4), "su3": _sb(384, U8),
+    "qv": _sb(128, Q4), "sv": _sb(128, U8), "qe": _sb(512, Q4), "se": _sb(512, U8),
+    "qw": _sb(512, Q4), "sw": _sb(512, U8),
+    "qj0": _sb(C, Q4), "sj0": _sb(C, U8), "qj1": _sb(C, Q4), "sj1": _sb(C, U8), "qj2": _sb(C, Q4), "sj2": _sb(C, U8),
+    "qz": _sb(C, Q4), "sz": _sb(C, U8),
+    "nbi": _sb(42, I32), "nb16": _sb(42, U16), "coli": _sb(4, I32), "colf": _sb(8, F32),
+    "uli": _sb(24, I32), "ul16": _sb(24, U16),
+    "r16": _sb(240, F32), "r4": _sb(C, F32), "jrow": _sb(C, F32), "jrow2": _sb(C, F32),
+    "mask": _sb(C, F32), "chold": _sb(240, F32), "cd": _sb(C, BF), "c32": _sb(C, F32), "ctmp": _sb(C, F32), "cb": _sb(C, BF),
+    "ct": _sb(42, F32), "jka": _sb(56, F32), "jkb": _sb(56, F32),
+    "rm": _sb(240, F32), "hh": _sb(240, F32), "mv": _sb(len(CV) * C, BF), "so": _sb(len(CV) * 112, BF),
+    "ta": _sb(len(CA) * C, BF), "eq": _sb(C, BF), "dg": _sb(C, BF), "tr": _sb(42, F32), "trs": _sb(42, F32),
+    "rk16": _sb(14, U16), "erow": _sb(C, F32), "es": _sb(K, F32),
+    "ww": _sb(768, F32), "dn": _sb(4 * C, F32), "keep": _sb(C, F32), "nm": _sb(C, F32),
+    "y0": _sb(C, F32), "y1": _sb(C, F32), "a0f": _sb(56, F32), "a1f": _sb(56, F32), "o0": _sb(56, U16), "o1": _sb(56, U16),
+    "s0": _sb(C, F32), "b01": _sb(C, F32), "m1": _sb(C, BF), "m2": _sb(C, BF), "ym1": _sb(C, BF), "ym2": _sb(C, BF),
+    "bt": _sb(56, F32), "b1": _sb(56, F32), "uu": _sb(56, F32), "vv": _sb(56, F32), "oz": _sb(56, U16), "ow": _sb(56, U16),
+    "rr": _sb(4 * C, F32), "ysb": _sb(C, F32), "opr": _sb(C, F32),
+}
+for _t in range(R + 1):
+    SCRATCH["qx%d" % _t] = _sb(C, Q4)
+    SCRATCH["sx%d" % _t] = _sb(C, U8)
+for _t in range(R):
+    SCRATCH["lq%d" % _t] = _sb(C, Q4)
+    SCRATCH["ls%d" % _t] = _sb(C, U8)
+    SCRATCH["ll%d" % _t] = _sb(16, U16)
+    SCRATCH["sl%d" % _t] = _sb(16, U16)
+for _t in range(8):
+    SCRATCH["ps%d" % _t] = ("psum", [128, 512], F32)
+
+SEMAPHORES = ["cv", "ca", "cp", "cg", "sent"] + ["d%d" % i for i in range(20)] \
+    + ["aq%d" % i for i in range(R)] + ["al%d" % i for i in range(R)]
+
+
+def rank_program(g, core, T, topo):
+    rank = T.rank_of(core)
+    if rank is None:
+        return
+    A_, ACT = AluOpType, ActivationFunctionType
+    nxt = T.cores[(rank + 1) % len(T.cores)]
+    prv = T.cores[(rank - 1) % len(T.cores)]
+    rid, pid, _se = topo.addr(nxt)
+    emask, ne_out, ne_in = topo.mask(core, nxt), len(topo.engines(core, nxt)), len(topo.engines(prv, core))
+
+    Q = {"V": g.vector, "A": g.scalar, "P": g.tensor, "S": g.sync, "G": g}
+    own = {"V": "cv", "A": "ca", "P": "cp", "G": "cg"}
+    clock = {k: {} for k in Q}
+    count = {}
+    wrote, readers = {}, {}
+    ndma = [0]
+
+    def wait(q, ev):
+        sem, val, snap = ev[0], ev[1], ev[2]
+        if clock[q].get(sem, 0) >= val:
+            return
+        Q[q].wait_ge(T.sem[sem], val)
+        clock[q][sem] = val
+        for s, v in snap.items():
+            if clock[q].get(s, 0) < v:
+                clock[q][s] = v
+
+    def order(q, reads, writes):
+        evs = []
+        for k in reads:
+            if k in wrote:
+                evs.append(wrote[k])
+            if k.startswith("ps"):
+                evs += [e for e in readers.get(k, []) if e[3] != q]
+        for k in writes:
+            if k in wrote:
+                evs.append(wrote[k])
+            evs += readers.get(k, [])
+        evs.sort(key=lambda e: -e[1])
+        for e in evs:
+            wait(q, e)
+
+    def note(ev, reads, writes):
+        for k in reads:
+            readers.setdefault(k, []).append(ev)
+        for k in writes:
+            wrote[k] = ev
+            readers[k] = []
+
+    def op(q, reads, writes, call):
+        order(q, reads, writes)
+        sem = own[q]
+        count[sem] = count.get(sem, 0) + 1
+        call().then_inc(T.sem[sem], 1)
+        note((sem, count[sem], dict(clock[q]), q), reads, writes)
+
+    def dma(q, reads, writes, out, in_):
+        order(q, reads, writes)
+        sem = "d%d" % ndma[0]
+        ndma[0] += 1
+        count[sem] = 16
+        Q[q].dma_start(out, in_).then_inc(T.sem[sem], 16)
+        note((sem, 16, dict(clock[q]), "D"), reads, writes)
+
+    def send(reads, out, in_, sem):
+        order("G", reads, [])
+        g.remote_dma(out, in_, T.sem[sem], T.sem.sent, pid, rid, emask)
+        count["sent"] = count.get("sent", 0) + ne_out
+
+    for t in range(R):
+        wrote["lq%d" % t] = ("aq%d" % t, 2 * ne_in, {}, "R")
+        wrote["ll%d" % t] = ("al%d" % t, ne_in, {}, "R")
+        count["aq%d" % t], count["al%d" % t] = 2 * ne_in, ne_in
+
+    V, S, PE = g.vector, g.scalar, g.tensor
+
+    def ts(reads, writes, out, in0, s1, s2, op0, op1=None):
+        if op1 is None:
+            op("V", reads, writes, lambda: V.tensor_scalar(out, in0, s1, None, op0))
+        else:
+            op("V", reads, writes, lambda: V.tensor_scalar(out, in0, s1, s2, op0, op1))
+
+    def tt(reads, writes, out, in0, in1, o):
+        op("V", reads, writes, lambda: V.tensor_tensor(out, in0, in1, o))
+
+    def scan(reads, writes, out, d0, d1, init, op0, op1):
+        op("V", reads, writes, lambda: V.tensor_tensor_scan(out, d0, d1, init, op0, op1))
+
+    def cp(reads, writes, out, in_):
+        op("V", reads, writes, lambda: V.tensor_copy(out, in_))
+
+    def ms(writes, ap, c):
+        op("V", [], writes, lambda: V.memset(ap, c))
+
+    def quant(reads, name, tile):
+        op("V", reads, ["q" + name], lambda: V.quantize_mx(T["q" + name][:], T["s" + name][:], tile))
+
+    def act(reads, writes, out, in_, func, **kw):
+        op("A", reads, writes, lambda: S.activation(out, in_, func, **kw))
+
+    def mm(bank, reads, wq, ws, xq, xs):
+        op("P", reads, ["ps%d" % bank],
+           lambda: PE.matmul_mx(T["ps%d" % bank][:, 0:C], wq, ws, xq, xs, True, True))
+
+    def mmu(bank, r, name):
+        mm(bank, ["qu3_%d" % r, "su3_%d" % r, "q" + name], T.qu3[:, 128 * r:128 * r + 128], T.su3[:, 128 * r:128 * r + 128],
+           T["q" + name][:], T["s" + name][:])
+
+    def iota(writes, out, pattern, base, cm, flt=True):
+        if flt:
+            op("G", [], writes, lambda: g.iota(out, pattern, base, cm, allow_small_or_imprecise_dtypes=True))
+        else:
+            op("G", [], writes, lambda: g.iota(out, pattern, base, cm))
+
+    def ps(b):
+        return T["ps%d" % b][:, 0:C]
+
+    def col(i):
+        return T.colf[:, i:i + 1]
+
+    XK = ["X0", "X1", "X2", "X3"]
+    J2K = ["J2_0", "J2_1", "J2_2", "J2_3"]
+    DK = ["dd0", "dd1", "dd2", "dd3"]
+    X = T.xs[:]
+
+    def pick_codes(r):
+        op("V", ["qu", "ul16"], ["qu3_%d" % r], lambda: V.tensor_copy(
+            T.qu3[:, 128 * r:128 * r + 128].bitcast(dt.uint32), T.qu[:, 0:128].bitcast(dt.uint32).indirect(T.ul16[:, 8 * r:8 * r + 8])))
+
+    def pick_scales(r):
+        act(["qu", "ul16"], ["su3_%d" % r], T.su3[:, 128 * r:128 * r + 128], T.su[:, 0:128].indirect(T.ul16[:, 8 * r:8 * r + 8]), ACT.Copy)
+
+    def n_minus_j(t, key, out):
+        tt(["jrow", "jrow2", "nb16"], [key], out, T.jrow[:, 0:C].indirect(T.nb16[:, 14 * t:14 * t + 14]), T.jrow2[:], A_.subtract)
+
+    dma("S", [], XK, X, T.x[:])
+    dma("A", [], ["ut"], T.ut[:], T.u[:])
+    dma("S", [], ["nbi"], T.nbi[:], T.nb[:])
+    dma("S", [], ["XP"], T.pool[:, 0:4 * C], T.x[:])
+    dma("S", [], ["J0"], T.jw[:, 0:4 * C], T.x[:])
+    dma("S", [], ["vt"], T.vt[:], T.v[:])
+    dma("S", [], ["qw"], T.qw[:].bitcast(dt.uint8), T.wc[:])
+    dma("S", [], ["sw"], T.sw[:], T.ws[:])
+
+    iota(["coli0"], T.coli[:, 0:1], [[0, 1]], 0, 1, False)
+    iota(["uli"], T.uli[:], [[1, 3], [16, 8]], 0, 0, False)
+    iota(["r16"], T.r16[:], [[0, 15], [1, 16]], 0, 0)
+    iota(["jrow"], T.jrow[:], [[1, C]], 0, 0)
+    iota(["r4"], T.r4[:], [[0, 56], [1, 4]], 0, 0)
+    ms(["et"], T.et[:], 0.0)
+    ts(["coli0"], ["coli1"], T.coli[:, 1:2], T.coli[:, 0:1], 15, None, A_.bitwise_and)
+    ts(["coli0"], ["coli2"], T.coli[:, 2:3], T.coli[:, 0:1], 15, 2, A_.bitwise_and, A_.logical_shift_right)
+    ts(["coli0"], ["coli3"], T.coli[:, 3:4], T.coli[:, 0:1], 3, None, A_.bitwise_and)
+    ms(["rmt"], T.rm[:, C:240], 0.0)
+    cp(["coli0", "coli1", "coli2", "coli3"], ["colf"], T.colf[:, 0:4], T.coli[:, 0:4])
+    cp(["uli"], ["ul16"], T.ul16[:], T.uli[:])
+    ms(["tr"], T.tr[:], 0.0)
+    ms(["ct"], T.ct[:], 1.0)
+    ts(["r16", "colf"], ["mask"], T.mask[:], T.r16[:, 0:C], col(1), None, A_.is_equal)
+    ts(["r16", "colf"], ["chold"], T.chold[:], T.r16[:], col(1), None, A_.not_equal)
+    ms(["ct"], T.ct[:, 0:42:3], 0.0)
+    quant(["ut"], "u", T.ut[:])
+    quant(XK, "x0", X)
+    pick_codes(0)
+    pick_scales(0)
+    ts(["mask"], ["cd"], T.cd[:], T.mask[:], 255.0, 1.0, A_.mult, A_.add)
+    ts(["colf"], ["colk"], col(4), col(2), -1024.0, 3072.0, A_.mult, A_.add)
+    ms(["cd"], T.cd[:, 0:C:16], 0.0)
+
+    for t in range(R):
+        qx = "x%d" % t
+        lq, ls, ll, sl = T["lq%d" % t], T["ls%d" % t], T["ll%d" % t], T["sl%d" % t]
+        send(["q" + qx], lq[:].bitcast(dt.uint8), T["q" + qx][:].bitcast(dt.uint8), "aq%d" % t)
+        send(["q" + qx], ls[:], T["s" + qx][:], "aq%d" % t)
+        if t == 0:
+            iota(["jrow2"], T.jrow2[:], [[1, C]], 0, 0)
+        iota(["W2"], T.ww[:, 512:768], [[-K, 4], [0, K]], C + K * t, 0)
+        mmu(0, 0, qx)
+        mmu(1, 0, qx)
+        if t:
+            mmu(2, 2, qx)
+
+        tt(["ps0", "mask"], ["rm"], T.rm[:, 0:C], ps(0), T.mask[:], A_.mult)
+        scan(["chold", "rm", "rmt"], ["hh"], T.hh[:], T.chold[:], T.rm[:], 0.0, A_.mult, A_.add)
+
+        for n, c in enumerate(CA):
+            act(["ps1", "hh"], ["ta%d" % n], T.ta[:, C * n:C * n + C], ps(1), ACT.Sign, bias=T.hh[:, 16 * c + 15:16 * c + 16], scale=-1.0)
+        for n, c in enumerate(CA):
+            a = T.ta[:, C * n + 16 * c:C * n + C]
+            act(["ta%d" % n, "tr"], ["tah%d" % n, "tr0_%d" % c], a, a, ACT.Sign, bias=-0.5, scale=-1.0, accum_out=T.tr[:, 3 * c:3 * c + 1])
+            if c:
+                a = T.ta[:, C * n:C * n + 16 * c]
+                act(["ta%d" % n, "tr"], ["tal%d" % n, "tr1_%d" % c], a, a, ACT.Sign, bias=0.5, scale=-1.0, accum_out=T.tr[:, 3 * c + 1:3 * c + 2])
+
+        for n, c in enumerate(CV):
+            h = T.hh[:, 16 * c + 15:16 * c + 16]
+            ts(["ps0", "hh"], ["mvl%d" % n], T.mv[:, C * n:C * n + 16 * c], T.ps0[:, 0:16 * c], h, 2.0, A_.is_ge, A_.mult)
+            ts(["ps0", "hh"], ["mvh%d" % n], T.mv[:, C * n + 16 * c:C * n + C], T.ps0[:, 16 * c:C], h, 2.0, A_.is_gt, A_.mult)
+        tt(["ps0", "hh"], ["eq"], T.eq[:], ps(0), T.hh[:, 16:240], A_.is_equal)
+        for n, c in enumerate(CV):
+            scan(["mvl%d" % n, "mvh%d" % n], ["so%d" % n], T.so[:, 112 * n:112 * n + 112],
+                 T.mv[:, C * n:C * n + 112], T.mv[:, C * n + 112:C * n + C], -float(C), A_.add, A_.add)
+        if t == 0:
+            pick_codes(1)
+        else:
+            ts(["ps2"], ["keep"], T.keep[:], ps(2), 0.0, None, A_.is_ge)
+        scan(["cd", "eq"], ["dg"], T.dg[:], T.cd[:], T.eq[:], 0.0, A_.mult, A_.add)
+        cp(["so%d" % n for n in range(len(CV))] + ["tr"], ["trv"],
+           T.tr[:, 3 * CV[0]:3 * CV[-1] + 1:3], T.so[:, 111:112 * len(CV):112])
+
+        w0, w1 = T.ww[:, 0:C], T.ww[:, 256:256 + C]
+        win = T.pool[:, 0:4 * C + 4 * K * t]
+        GK = ["XP"] + ["G%d" % i for i in range(t)]
+        if t == 0:
+            ts(["r4", "colf"], ["c32"], T.c32[:], T.r4[:], col(2), 8192.0, A_.is_equal, A_.mult)
+            ts(["r4", "colf"], ["ctmp"], T.ctmp[:], T.r4[:], col(2), -1024.0, A_.is_gt, A_.mult)
+            ts(["dg", "tr"], ["tr2"], T.tr[:, 2:42:3], T.dg[:, 15:C:16], 1.0 / 128, None, A_.mult)
+            ts(["colk", "colf"], ["cole"], col(5), col(4), 4.0, col(3), A_.mult, A_.add)
+            ts(["colk"], ["colh"], col(6), col(4), -1.0 / 1024, None, A_.mult)
+            ts(["jrow", "colf", "colk"], ["jka"], T.jka[:], T.jrow[:, 0:C:4], col(2), col(4), A_.add, A_.add)
+            cp(["nbi"], ["nb16"], T.nb16[:], T.nbi[:])
+            tt(["c32", "ctmp"], ["c32"], T.c32[:], T.c32[:], T.ctmp[:], A_.add)
+            for b in range(4):
+                ts(["jrow", "colf", "et"], ["et%d" % b], T.et[:, 512 * b + b:512 * b + 512:4], T.jrow[:, 0:128], col(0), None, A_.is_equal)
+            n_minus_j(0, "W1", w1)
+            quant(["et%d" % b for b in range(4)], "e", T.et[:])
+            scan(["c32", "W1"], ["y1"], T.y1[:], T.c32[:], w1, 0.0, A_.add, A_.min)
+            ms(["W0"], T.ww[:, 0:256], 0.0)
+            tt(["y1", "jka"], ["a1f"], T.a1f[:], T.y1[:, 3:C:4], T.jka[:], A_.add)
+            ms(["Wg"], T.ww[:, 256 + C:512], 0.0)
+            ts(["a1f", "colf"], ["o1"], T.o1[:], T.a1f[:], 4.0, col(3), A_.mult, A_.add)
+        else:
+            tt(["keep", "dn"], ["W0"], w0, T.keep[:], T.dn[:, 0:4 * C:4], A_.mult)
+            ts(["dg", "tr"], ["tr2"], T.tr[:, 2:42:3], T.dg[:, 15:C:16], 1.0 / 128, None, A_.mult)
+            scan(["c32", "W0"], ["y0"], T.y0[:], T.c32[:], w0, 0.0, A_.add, A_.min)
+            tt(["W0", "nb16", "nm"], ["W1"], w1, w0.indirect(T.nb16[:, 14 * t:14 * t + 14]), T.nm[:], A_.add)
+            tt(["y0", "jka"], ["a0f"], T.a0f[:], T.y0[:, 3:C:4], T.jka[:], A_.add)
+            scan(["c32", "W1"], ["y1"], T.y1[:], T.c32[:], w1, 0.0, A_.add, A_.min)
+            ts(["a0f", "colf"], ["o0"], T.o0[:], T.a0f[:], 4.0, col(3), A_.mult, A_.add)
+            tt(["y1", "jka"], ["a1f"], T.a1f[:], T.y1[:, 3:C:4], T.jka[:], A_.add)
+            tt(XK + GK + ["o0"], ["J0"], T.jw[:, 0:4 * C], win.indirect(T.o0[:]), X, A_.max)
+            ts(["a1f", "colf"], ["o1"], T.o1[:], T.a1f[:], 4.0, col(3), A_.mult, A_.add)
+            quant(["J0"], "j0", T.jw[:, 0:4 * C])
+
+        trk = ["tr0_%d" % c for c in CA] + ["tr1_%d" % c for c in CA if c] + ["trv", "tr2", "tr"]
+        scan(trk + ["ct"], ["trs"], T.trs[:], T.ct[:], T.tr[:], 0.0, A_.mult, A_.add)
+        ts(["trs"], ["rk16"], T.rk16[:], T.trs[:, 2:42:3], 0.5, C / 2 + 0.25, A_.mult, A_.add)
+        cp(["rk16", "jrow"], ["erow"], T.erow[:, 0:C].indirect(T.rk16[:]), T.jrow[:])
+        scan(["c32", "erow"], ["es"], T.es[:], T.c32[:, 0:K], T.erow[:, 0:K], 0.0, A_.add, A_.min)
+        ts(["es", "cole"], ["sl%d" % t], sl[:], T.es[:, 3:K:4], 4.0, col(5), A_.mult, A_.add)
+        send(["sl%d" % t], ll[:], sl[:], "al%d" % t)
+
+        if t == 0:
+            pick_scales(1)
+        for b in range(4):
+            mm(4 + b, ["qe", "lq%d" % t], T.qe[:, 128 * b:128 * b + 128], T.se[:, 128 * b:128 * b + 128], lq[:], ls[:])
+        mmu(3, 1, "j0" if t else qx)
+        for b in range(4):
+            act(["ps%d" % (4 + b)], [DK[b]], T.dd[:, b:4 * C:4], ps(4 + b), ACT.Copy)
+        act(["ps3"], ["s0"], T.s0[:], ps(3), ACT.Copy)
+        if t == 0:
+            pick_scales(2)
+
+        tt(XK + GK + ["o1"], ["J1"], T.jw[:, 1024:1024 + 4 * C], win.indirect(T.o1[:]), X, A_.max)
+        quant(["J1"], "j1", T.jw[:, 1024:1024 + 4 * C])
+        mmu(2, 1, "j1")
+        if t == 0:
+            ts(["c32"], ["cb"], T.cb[:], T.c32[:], 1.0 / 512, None, A_.mult)
+            ts(["jka"], ["jkb"], T.jkb[:], T.jka[:], 1.0 / 512, None, A_.mult)
+            ms(["jg0"], T.jw[:, 4 * C:1024], 0.0)
+            ms(["jg1"], T.jw[:, 1024 + 4 * C:2048], 0.0)
+            pick_codes(2)
+
+        for i in range(4):
+            w = min(4 * K, 4 * C - 4 * K * i)
+            tt(XK + DK + ["ll%d" % t], [J2K[i]], T.jw[:, 2048 + 256 * i:2048 + 256 * i + w],
+               T.dd[:, 0:4 * C].indirect(ll[:, 0:w // 16]), T.xs[:, 256 * i:256 * i + w], A_.max)
+        if t + 1 < R:
+            act(DK + ["ll%d" % t], ["G%d" % t], T.pool[:, 4 * C + 256 * t:4 * C + 256 * t + 256], T.dd[:, 0:4 * C].indirect(ll[:]), ACT.Copy)
+        quant(J2K, "j2", T.jw[:, 2048:2048 + 4 * C])
+        mmu(0, 1, "j2")
+
+        tt(["ps2", "s0"], ["m1"], T.m1[:], ps(2), T.s0[:], A_.is_gt)
+        tt(["ps2", "s0"], ["b01"], T.b01[:], ps(2), T.s0[:], A_.max)
+        scan(["cb", "m1"], ["ym1"], T.ym1[:], T.cb[:], T.m1[:], 0.0, A_.add, A_.min)
+        tt(["ps0", "b01"], ["m2"], T.m2[:], ps(0), T.b01[:], A_.is_gt)
+        ts(["ym1", "colh"], ["bt"], T.bt[:], T.ym1[:, 3:C:4], 0.5, col(6), A_.mult, A_.add)
+        scan(["cb", "m2"], ["ym2"], T.ym2[:], T.cb[:], T.m2[:], 0.0, A_.add, A_.min)
+        tt(["bt", "jkb"], ["b1"], T.b1[:], T.bt[:], T.jkb[:], A_.add)
+        tt(["ym2", "jkb"], ["uu"], T.uu[:], T.ym2[:, 3:C:4], T.jkb[:], A_.add)
+        tt(["uu", "b1"], ["vv"], T.vv[:], T.uu[:], T.b1[:], A_.max)
+        ts(["vv", "colf"], ["oz"], T.oz[:], T.vv[:], 2048.0, col(3), A_.mult, A_.add)
+        JK = ["J0", "J1", "jg0", "jg1", "oz"] + J2K
+        jwin = T.jw[:, 0:2048 + 4 * C]
+        act(JK, ["zb"], T.zt[:, 448:896], jwin.indirect(T.oz[:, 28:56]), ACT.Copy)
+        cp(JK, ["za"], T.zt[:, 0:448], jwin.indirect(T.oz[:, 0:28]))
+        ts(["vv"], ["ow"], T.ow[:], T.vv[:], 512.0, None, A_.mult)
+        quant(["za", "zb"], "z", T.zt[:])
+        if t + 1 < R:
+            n_minus_j(t + 1, "nm", T.nm[:])
+        if t == 0:
+            quant(["vt"], "v", T.vt[:])
+
+        for b in range(4):
+            mm(4 + b, ["qw", "sw", "qz"], T.qw[:, 128 * b:128 * b + 128], T.sw[:, 128 * b:128 * b + 128], T.qz[:], T.sz[:])
+        for b in range(4):
+            act(["ps%d" % (4 + b)], ["rr%d" % b], T.rr[:, C * b:C * b + C], ps(4 + b), ACT.Relu, scale=0.015625)
+        act(["W0", "W1", "W2", "Wg", "ow"], ["dn"], T.dn[:], T.ww[:, 0:768].indirect(T.ow[:]), ACT.Copy)
+        for b in range(4):
+            xb = T.xs[:, b:4 * C:4]
+            tt(["rr%d" % b, XK[b]], [XK[b]], xb, T.rr[:, C * b:C * b + C], xb, A_.add)
+        quant(XK, "x%d" % (t + 1), X)
+        if t + 1 < R:
+            dma("S", XK, ["XP"], T.pool[:, 0:4 * C], X)
+
+    qx = "x%d" % R
+    mm(1, ["qv", "q" + qx], T.qv[:], T.sv[:], T["q" + qx][:], T["s" + qx][:])
+    tt(["dn", "jrow"], ["opr"], T.opr[:], T.dn[:, 0:4 * C:4], T.jrow[:], A_.add)
+    dma("S", ["q" + qx], [], T.oc[:], T["q" + qx][:].bitcast(dt.uint8))
+    for k in range(4):
+        dma("S", ["q" + qx], [], T.osc[4 * k:4 * k + 4, 0:C], T["s" + qx][32 * k:32 * k + 4, 0:C])
+    act(["ps1"], ["ysb"], T.ysb[:], ps(1), ACT.Copy)
+    dma("A", ["ysb"], [], T.y[:], T.ysb[:])
+    dma("S", ["opr"], [], T.op[:], T.opr[0:128:16, 0:C])
+
+    for sem, val in count.items():
+        wait("G", (sem, val, {}, "E"))

@@ -1,8 +1,7 @@
 from concourse.mybir import dt, AluOpType, ActivationFunctionType
 
 C, K, R = 224, 64, 3
-CV = [5, 6, 7, 8, 9]
-CA = [c for c in range(14) if c not in CV]
+CVS = [[4, 5, 6, 7, 8, 9, 10], [5, 6, 7, 8, 9], [5, 6, 7, 8, 9]]
 Q4, U8, BF, F32, I32, U16 = "float8_e4m3fn_x4", "uint8", "bfloat16", "float32", "int32", "uint16"
 
 
@@ -12,7 +11,7 @@ def _sb(n, d):
 
 SCRATCH = {
     "xs": _sb(4 * C, BF), "pool": _sb(4 * C + 2 * 4 * K, BF), "jw": _sb(3072, BF), "zt": _sb(4 * C, BF), "dd": _sb(4 * C, BF),
-    "ut": _sb(512, BF), "vt": _sb(512, BF), "et": _sb(2048, BF),
+    "ut": _sb(512, BF), "vt": _sb(512, BF), "et": _sb(2048, BF), "ones": _sb(128, BF),
     "qu": _sb(128, Q4), "su": _sb(128, U8), "qu3": _sb(384, Q4), "su3": _sb(384, U8),
     "qv": _sb(128, Q4), "sv": _sb(128, U8), "qe": _sb(512, Q4), "se": _sb(512, U8),
     "qw": _sb(512, Q4), "sw": _sb(512, U8),
@@ -23,8 +22,8 @@ SCRATCH = {
     "r16": _sb(240, F32), "r4": _sb(C, F32), "jrow": _sb(C, F32), "jrow2": _sb(C, F32),
     "mask": _sb(C, F32), "chold": _sb(240, F32), "cd": _sb(C, BF), "c32": _sb(C, F32), "ctmp": _sb(C, F32), "cb": _sb(C, BF),
     "ct": _sb(42, F32), "jka": _sb(56, F32), "jkb": _sb(56, F32),
-    "rm": _sb(240, F32), "hh": _sb(240, F32), "mv": _sb(len(CV) * C, BF), "so": _sb(len(CV) * 112, BF),
-    "ta": _sb(len(CA) * C, BF), "eq": _sb(C, BF), "dg": _sb(C, BF), "tr": _sb(42, F32), "trs": _sb(42, F32),
+    "rm": _sb(240, F32), "hh": _sb(240, F32), "mv": _sb(7 * C, BF), "so": _sb(7 * 112, BF),
+    "ta": _sb(10 * C, BF), "eq": _sb(C, BF), "dg": _sb(C, BF), "tr": _sb(42, F32), "trs": _sb(42, F32),
     "rk16": _sb(14, U16), "erow": _sb(C, F32), "es": _sb(K, F32),
     "ww": _sb(768, F32), "dn": _sb(4 * C, F32), "keep": _sb(C, F32), "nm": _sb(C, F32),
     "y0": _sb(C, F32), "y1": _sb(C, F32), "a0f": _sb(56, F32), "a1f": _sb(56, F32), "o0": _sb(56, U16), "o1": _sb(56, U16),
@@ -182,6 +181,10 @@ def rank_program(g, core, T, topo):
     def n_minus_j(t, key, out):
         tt(["jrow", "jrow2", "nb16"], [key], out, T.jrow[:, 0:C].indirect(T.nb16[:, 14 * t:14 * t + 14]), T.jrow2[:], A_.subtract)
 
+    def identity(b):
+        op("G", ["ones", "et"], ["et%d" % b], lambda: g.affine_select(
+            T.et[:, 512 * b + b:512 * b + 512:4], T.ones[:], [[-1, 128]], A_.is_equal, 0.0, 0, 1))
+
     dma("S", [], XK, X, T.x[:])
     dma("A", [], ["ut"], T.ut[:], T.u[:])
     dma("S", [], ["nbi"], T.nbi[:], T.nb[:])
@@ -193,47 +196,69 @@ def rank_program(g, core, T, topo):
 
     iota(["coli0"], T.coli[:, 0:1], [[0, 1]], 0, 1, False)
     iota(["uli"], T.uli[:], [[1, 3], [16, 8]], 0, 0, False)
+    iota(["r4"], T.r4[:], [[0, 56], [1, 4]], 0, 0)
     iota(["r16"], T.r16[:], [[0, 15], [1, 16]], 0, 0)
     iota(["jrow"], T.jrow[:], [[1, C]], 0, 0)
-    iota(["r4"], T.r4[:], [[0, 56], [1, 4]], 0, 0)
-    ms(["et"], T.et[:], 0.0)
+    ms(["ones"], T.ones[:], 1.0)
+    ms(["rmt"], T.rm[:, C:240], 0.0)
     ts(["coli0"], ["coli1"], T.coli[:, 1:2], T.coli[:, 0:1], 15, None, A_.bitwise_and)
     ts(["coli0"], ["coli2"], T.coli[:, 2:3], T.coli[:, 0:1], 15, 2, A_.bitwise_and, A_.logical_shift_right)
     ts(["coli0"], ["coli3"], T.coli[:, 3:4], T.coli[:, 0:1], 3, None, A_.bitwise_and)
-    ms(["rmt"], T.rm[:, C:240], 0.0)
+    ms(["ct"], T.ct[:], 1.0)
     cp(["coli0", "coli1", "coli2", "coli3"], ["colf"], T.colf[:, 0:4], T.coli[:, 0:4])
     cp(["uli"], ["ul16"], T.ul16[:], T.uli[:])
+    ms(["et"], T.et[:], 0.0)
     ms(["tr"], T.tr[:], 0.0)
-    ms(["ct"], T.ct[:], 1.0)
+    ts(["colf"], ["colk"], col(4), col(2), -1024.0, 3072.0, A_.mult, A_.add)
+    ts(["colf"], ["colj"], col(7), col(2), -1023.0, 3072.0, A_.mult, A_.add)
+    ms(["ct"], T.ct[:, 0:42:3], 0.0)
     ts(["r16", "colf"], ["mask"], T.mask[:], T.r16[:, 0:C], col(1), None, A_.is_equal)
     ts(["r16", "colf"], ["chold"], T.chold[:], T.r16[:], col(1), None, A_.not_equal)
-    ms(["ct"], T.ct[:, 0:42:3], 0.0)
+    act(["r4", "colf"], ["ctmp"], T.ctmp[:], T.r4[:], ACT.Sign, bias=col(2), scale=-1.0)
+    act(["ctmp"], ["ctmp"], T.ctmp[:], T.ctmp[:], ACT.Abs)
+    act(["ctmp"], ["c32"], T.c32[:], T.ctmp[:], ACT.Identity, bias=16384.0, scale=-17408.0)
+    for b in range(4):
+        identity(b)
     quant(["ut"], "u", T.ut[:])
     quant(XK, "x0", X)
     pick_codes(0)
     pick_scales(0)
+    act(["jrow"], ["jrow2"], T.jrow2[:], T.jrow[:], ACT.Copy)
+    act(["jrow", "colj"], ["jka"], T.jka[:], T.jrow[:, 0:C:4], ACT.Identity, bias=col(7))
     ts(["mask"], ["cd"], T.cd[:], T.mask[:], 255.0, 1.0, A_.mult, A_.add)
-    ts(["colf"], ["colk"], col(4), col(2), -1024.0, 3072.0, A_.mult, A_.add)
+    ts(["colk", "colf"], ["cole"], col(5), col(4), 4.0, col(3), A_.mult, A_.add)
     ms(["cd"], T.cd[:, 0:C:16], 0.0)
 
     for t in range(R):
+        CV = CVS[t]
+        CA = [c for c in range(14) if c not in CV]
         qx = "x%d" % t
         lq, ls, ll, sl = T["lq%d" % t], T["ls%d" % t], T["ll%d" % t], T["sl%d" % t]
+        w0, w1 = T.ww[:, 0:C], T.ww[:, 256:256 + C]
+        win = T.pool[:, 0:4 * C + 4 * K * t]
+        GK = ["XP"] + ["G%d" % i for i in range(t)]
         send(["q" + qx], lq[:].bitcast(dt.uint8), T["q" + qx][:].bitcast(dt.uint8), "aq%d" % t)
         send(["q" + qx], ls[:], T["s" + qx][:], "aq%d" % t)
-        if t == 0:
-            iota(["jrow2"], T.jrow2[:], [[1, C]], 0, 0)
         iota(["W2"], T.ww[:, 512:768], [[-K, 4], [0, K]], C + K * t, 0)
         mmu(0, 0, qx)
-        mmu(1, 0, qx)
         if t:
             mmu(2, 2, qx)
+        mmu(1, 0, qx)
 
         tt(["ps0", "mask"], ["rm"], T.rm[:, 0:C], ps(0), T.mask[:], A_.mult)
+        if t:
+            ts(["ps2"], ["keep"], T.keep[:], ps(2), 0.0, None, A_.is_ge)
+        else:
+            cp(["nbi"], ["nb16"], T.nb16[:], T.nbi[:])
         scan(["chold", "rm", "rmt"], ["hh"], T.hh[:], T.chold[:], T.rm[:], 0.0, A_.mult, A_.add)
+        if t:
+            tt(["keep", "dn"], ["W0"], w0, T.keep[:], T.dn[:, 0:4 * C:4], A_.mult)
+        else:
+            n_minus_j(0, "W1", w1)
 
         for n, c in enumerate(CA):
-            act(["ps1", "hh"], ["ta%d" % n], T.ta[:, C * n:C * n + C], ps(1), ACT.Sign, bias=T.hh[:, 16 * c + 15:16 * c + 16], scale=-1.0)
+            act(["ps1", "hh"], ["ta%d" % n, "tah%d" % n, "tal%d" % n], T.ta[:, C * n:C * n + C], ps(1), ACT.Sign,
+                bias=T.hh[:, 16 * c + 15:16 * c + 16], scale=-1.0)
         for n, c in enumerate(CA):
             a = T.ta[:, C * n + 16 * c:C * n + C]
             act(["ta%d" % n, "tr"], ["tah%d" % n, "tr0_%d" % c], a, a, ACT.Sign, bias=-0.5, scale=-1.0, accum_out=T.tr[:, 3 * c:3 * c + 1])
@@ -241,61 +266,54 @@ def rank_program(g, core, T, topo):
                 a = T.ta[:, C * n:C * n + 16 * c]
                 act(["ta%d" % n, "tr"], ["tal%d" % n, "tr1_%d" % c], a, a, ACT.Sign, bias=0.5, scale=-1.0, accum_out=T.tr[:, 3 * c + 1:3 * c + 2])
 
-        for n, c in enumerate(CV):
+        def compare(n):
+            c = CV[n]
             h = T.hh[:, 16 * c + 15:16 * c + 16]
             ts(["ps0", "hh"], ["mvl%d" % n], T.mv[:, C * n:C * n + 16 * c], T.ps0[:, 0:16 * c], h, 2.0, A_.is_ge, A_.mult)
             ts(["ps0", "hh"], ["mvh%d" % n], T.mv[:, C * n + 16 * c:C * n + C], T.ps0[:, 16 * c:C], h, 2.0, A_.is_gt, A_.mult)
+
         tt(["ps0", "hh"], ["eq"], T.eq[:], ps(0), T.hh[:, 16:240], A_.is_equal)
-        for n, c in enumerate(CV):
+        compare(0)
+        if t:
+            scan(["c32", "W0"], ["y0"], T.y0[:], T.c32[:], w0, 0.0, A_.add, A_.min)
+        scan(["cd", "eq"], ["dg"], T.dg[:], T.cd[:], T.eq[:], 0.0, A_.mult, A_.add)
+        compare(1)
+        if t:
+            tt(["y0", "jka"], ["a0f"], T.a0f[:], T.y0[:, 3:C:4], T.jka[:], A_.add)
+        ts(["dg", "tr"], ["tr2"], T.tr[:, 2:42:3], T.dg[:, 15:C:16], 1.0 / 128, None, A_.mult)
+        compare(2)
+        if t:
+            ts(["a0f", "colf"], ["o0"], T.o0[:], T.a0f[:], 4.0, col(3), A_.mult, A_.add)
+        for n in range(3, len(CV)):
+            compare(n)
+        if t:
+            tt(["W0", "nb16", "nm"], ["W1"], w1, w0.indirect(T.nb16[:, 14 * t:14 * t + 14]), T.nm[:], A_.add)
+        else:
+            pick_codes(1)
+        for n in range(len(CV)):
             scan(["mvl%d" % n, "mvh%d" % n], ["so%d" % n], T.so[:, 112 * n:112 * n + 112],
                  T.mv[:, C * n:C * n + 112], T.mv[:, C * n + 112:C * n + C], -float(C), A_.add, A_.add)
-        if t == 0:
-            pick_codes(1)
-        else:
-            ts(["ps2"], ["keep"], T.keep[:], ps(2), 0.0, None, A_.is_ge)
-        scan(["cd", "eq"], ["dg"], T.dg[:], T.cd[:], T.eq[:], 0.0, A_.mult, A_.add)
-        cp(["so%d" % n for n in range(len(CV))] + ["tr"], ["trv"],
-           T.tr[:, 3 * CV[0]:3 * CV[-1] + 1:3], T.so[:, 111:112 * len(CV):112])
-
-        w0, w1 = T.ww[:, 0:C], T.ww[:, 256:256 + C]
-        win = T.pool[:, 0:4 * C + 4 * K * t]
-        GK = ["XP"] + ["G%d" % i for i in range(t)]
-        if t == 0:
-            ts(["r4", "colf"], ["c32"], T.c32[:], T.r4[:], col(2), 8192.0, A_.is_equal, A_.mult)
-            ts(["r4", "colf"], ["ctmp"], T.ctmp[:], T.r4[:], col(2), -1024.0, A_.is_gt, A_.mult)
-            ts(["dg", "tr"], ["tr2"], T.tr[:, 2:42:3], T.dg[:, 15:C:16], 1.0 / 128, None, A_.mult)
-            ts(["colk", "colf"], ["cole"], col(5), col(4), 4.0, col(3), A_.mult, A_.add)
-            ts(["colk"], ["colh"], col(6), col(4), -1.0 / 1024, None, A_.mult)
-            ts(["jrow", "colf", "colk"], ["jka"], T.jka[:], T.jrow[:, 0:C:4], col(2), col(4), A_.add, A_.add)
-            cp(["nbi"], ["nb16"], T.nb16[:], T.nbi[:])
-            tt(["c32", "ctmp"], ["c32"], T.c32[:], T.c32[:], T.ctmp[:], A_.add)
-            for b in range(4):
-                ts(["jrow", "colf", "et"], ["et%d" % b], T.et[:, 512 * b + b:512 * b + 512:4], T.jrow[:, 0:128], col(0), None, A_.is_equal)
-            n_minus_j(0, "W1", w1)
-            quant(["et%d" % b for b in range(4)], "e", T.et[:])
-            scan(["c32", "W1"], ["y1"], T.y1[:], T.c32[:], w1, 0.0, A_.add, A_.min)
-            ms(["W0"], T.ww[:, 0:256], 0.0)
-            tt(["y1", "jka"], ["a1f"], T.a1f[:], T.y1[:, 3:C:4], T.jka[:], A_.add)
-            ms(["Wg"], T.ww[:, 256 + C:512], 0.0)
-            ts(["a1f", "colf"], ["o1"], T.o1[:], T.a1f[:], 4.0, col(3), A_.mult, A_.add)
-        else:
-            tt(["keep", "dn"], ["W0"], w0, T.keep[:], T.dn[:, 0:4 * C:4], A_.mult)
-            ts(["dg", "tr"], ["tr2"], T.tr[:, 2:42:3], T.dg[:, 15:C:16], 1.0 / 128, None, A_.mult)
-            scan(["c32", "W0"], ["y0"], T.y0[:], T.c32[:], w0, 0.0, A_.add, A_.min)
-            tt(["W0", "nb16", "nm"], ["W1"], w1, w0.indirect(T.nb16[:, 14 * t:14 * t + 14]), T.nm[:], A_.add)
-            tt(["y0", "jka"], ["a0f"], T.a0f[:], T.y0[:, 3:C:4], T.jka[:], A_.add)
-            scan(["c32", "W1"], ["y1"], T.y1[:], T.c32[:], w1, 0.0, A_.add, A_.min)
-            ts(["a0f", "colf"], ["o0"], T.o0[:], T.a0f[:], 4.0, col(3), A_.mult, A_.add)
-            tt(["y1", "jka"], ["a1f"], T.a1f[:], T.y1[:, 3:C:4], T.jka[:], A_.add)
+        if t:
             tt(XK + GK + ["o0"], ["J0"], T.jw[:, 0:4 * C], win.indirect(T.o0[:]), X, A_.max)
-            ts(["a1f", "colf"], ["o1"], T.o1[:], T.a1f[:], 4.0, col(3), A_.mult, A_.add)
-            quant(["J0"], "j0", T.jw[:, 0:4 * C])
+        else:
+            quant(["et%d" % b for b in range(4)], "e", T.et[:])
+        cp(["so%d" % n for n in range(len(CV))] + ["tr"], ["tr0_%d" % c for c in CV],
+           T.tr[:, 3 * CV[0]:3 * CV[-1] + 1:3], T.so[:, 111:112 * len(CV):112])
+        scan(["c32", "W1"], ["y1"], T.y1[:], T.c32[:], w1, 0.0, A_.add, A_.min)
 
-        trk = ["tr0_%d" % c for c in CA] + ["tr1_%d" % c for c in CA if c] + ["trv", "tr2", "tr"]
+        trk = ["tr0_%d" % c for c in range(14)] + ["tr1_%d" % c for c in CA if c] + ["tr2", "tr"]
         scan(trk + ["ct"], ["trs"], T.trs[:], T.ct[:], T.tr[:], 0.0, A_.mult, A_.add)
+        tt(["y1", "jka"], ["a1f"], T.a1f[:], T.y1[:, 3:C:4], T.jka[:], A_.add)
         ts(["trs"], ["rk16"], T.rk16[:], T.trs[:, 2:42:3], 0.5, C / 2 + 0.25, A_.mult, A_.add)
+        ts(["a1f", "colf"], ["o1"], T.o1[:], T.a1f[:], 4.0, col(3), A_.mult, A_.add)
         cp(["rk16", "jrow"], ["erow"], T.erow[:, 0:C].indirect(T.rk16[:]), T.jrow[:])
+        if t:
+            quant(["J0"], "j0", T.jw[:, 0:4 * C])
+        else:
+            ms(["jg0"], T.jw[:, 4 * C:1024], 0.0)
         scan(["c32", "erow"], ["es"], T.es[:], T.c32[:, 0:K], T.erow[:, 0:K], 0.0, A_.add, A_.min)
+        if t == 0:
+            ms(["jg1"], T.jw[:, 1024 + 4 * C:2048], 0.0)
         ts(["es", "cole"], ["sl%d" % t], sl[:], T.es[:, 3:K:4], 4.0, col(5), A_.mult, A_.add)
         send(["sl%d" % t], ll[:], sl[:], "al%d" % t)
 
@@ -308,17 +326,18 @@ def rank_program(g, core, T, topo):
             act(["ps%d" % (4 + b)], [DK[b]], T.dd[:, b:4 * C:4], ps(4 + b), ACT.Copy)
         act(["ps3"], ["s0"], T.s0[:], ps(3), ACT.Copy)
         if t == 0:
+            act(["ctmp"], ["cb"], T.cb[:], T.ctmp[:], ACT.Identity, bias=32.0, scale=-34.0)
+            act(["jka"], ["jkb"], T.jkb[:], T.jka[:], ACT.Copy, scale=1.0 / 512)
             pick_scales(2)
 
         tt(XK + GK + ["o1"], ["J1"], T.jw[:, 1024:1024 + 4 * C], win.indirect(T.o1[:]), X, A_.max)
+        if t == 0:
+            ms(["W0"], T.ww[:, 0:256], 0.0)
         quant(["J1"], "j1", T.jw[:, 1024:1024 + 4 * C])
         mmu(2, 1, "j1")
         if t == 0:
-            ts(["c32"], ["cb"], T.cb[:], T.c32[:], 1.0 / 512, None, A_.mult)
-            ts(["jka"], ["jkb"], T.jkb[:], T.jka[:], 1.0 / 512, None, A_.mult)
-            ms(["jg0"], T.jw[:, 4 * C:1024], 0.0)
-            ms(["jg1"], T.jw[:, 1024 + 4 * C:2048], 0.0)
-            pick_codes(2)
+            ts(["colk"], ["colh"], col(6), col(4), -1.0 / 1024, None, A_.mult)
+            ms(["Wg"], T.ww[:, 256 + C:512], 0.0)
 
         for i in range(4):
             w = min(4 * K, 4 * C - 4 * K * i)
@@ -326,10 +345,10 @@ def rank_program(g, core, T, topo):
                T.dd[:, 0:4 * C].indirect(ll[:, 0:w // 16]), T.xs[:, 256 * i:256 * i + w], A_.max)
         if t + 1 < R:
             act(DK + ["ll%d" % t], ["G%d" % t], T.pool[:, 4 * C + 256 * t:4 * C + 256 * t + 256], T.dd[:, 0:4 * C].indirect(ll[:]), ACT.Copy)
+        tt(["ps2", "s0"], ["m1"], T.m1[:], ps(2), T.s0[:], A_.is_gt)
         quant(J2K, "j2", T.jw[:, 2048:2048 + 4 * C])
         mmu(0, 1, "j2")
 
-        tt(["ps2", "s0"], ["m1"], T.m1[:], ps(2), T.s0[:], A_.is_gt)
         tt(["ps2", "s0"], ["b01"], T.b01[:], ps(2), T.s0[:], A_.max)
         scan(["cb", "m1"], ["ym1"], T.ym1[:], T.cb[:], T.m1[:], 0.0, A_.add, A_.min)
         tt(["ps0", "b01"], ["m2"], T.m2[:], ps(0), T.b01[:], A_.is_gt)
@@ -339,15 +358,15 @@ def rank_program(g, core, T, topo):
         tt(["ym2", "jkb"], ["uu"], T.uu[:], T.ym2[:, 3:C:4], T.jkb[:], A_.add)
         tt(["uu", "b1"], ["vv"], T.vv[:], T.uu[:], T.b1[:], A_.max)
         ts(["vv", "colf"], ["oz"], T.oz[:], T.vv[:], 2048.0, col(3), A_.mult, A_.add)
+        ts(["vv"], ["ow"], T.ow[:], T.vv[:], 512.0, None, A_.mult)
         JK = ["J0", "J1", "jg0", "jg1", "oz"] + J2K
         jwin = T.jw[:, 0:2048 + 4 * C]
         act(JK, ["zb"], T.zt[:, 448:896], jwin.indirect(T.oz[:, 28:56]), ACT.Copy)
         cp(JK, ["za"], T.zt[:, 0:448], jwin.indirect(T.oz[:, 0:28]))
-        ts(["vv"], ["ow"], T.ow[:], T.vv[:], 512.0, None, A_.mult)
         quant(["za", "zb"], "z", T.zt[:])
         if t + 1 < R:
             n_minus_j(t + 1, "nm", T.nm[:])
-        if t == 0:
+        else:
             quant(["vt"], "v", T.vt[:])
 
         for b in range(4):
@@ -355,6 +374,8 @@ def rank_program(g, core, T, topo):
         for b in range(4):
             act(["ps%d" % (4 + b)], ["rr%d" % b], T.rr[:, C * b:C * b + C], ps(4 + b), ACT.Relu, scale=0.015625)
         act(["W0", "W1", "W2", "Wg", "ow"], ["dn"], T.dn[:], T.ww[:, 0:768].indirect(T.ow[:]), ACT.Copy)
+        if t == 0:
+            pick_codes(2)
         for b in range(4):
             xb = T.xs[:, b:4 * C:4]
             tt(["rr%d" % b, XK[b]], [XK[b]], xb, T.rr[:, C * b:C * b + C], xb, A_.add)
@@ -370,7 +391,7 @@ def rank_program(g, core, T, topo):
         dma("S", ["q" + qx], [], T.osc[4 * k:4 * k + 4, 0:C], T["s" + qx][32 * k:32 * k + 4, 0:C])
     act(["ps1"], ["ysb"], T.ysb[:], ps(1), ACT.Copy)
     dma("A", ["ysb"], [], T.y[:], T.ysb[:])
-    dma("S", ["opr"], [], T.op[:], T.opr[0:128:16, 0:C])
+    dma("A", ["opr"], [], T.op[:], T.opr[0:128:16, 0:C])
 
     for sem, val in count.items():
         wait("G", (sem, val, {}, "E"))

from concourse.mybir import dt, AluOpType, ActivationFunctionType

C, K, R = 224, 64, 3
CVS = [[4, 5, 6, 7, 8, 9, 10], [5, 6, 7, 8, 9], [5, 6, 7, 8, 9]]
Q4, U8, BF, F32, I32, U16 = "float8_e4m3fn_x4", "uint8", "bfloat16", "float32", "int32", "uint16"


def _sb(n, d):
    return ("sbuf", [128, n], d)


SCRATCH = {
    "xs": _sb(4 * C, BF), "pool": _sb(4 * C + 2 * 4 * K, BF), "jw": _sb(3072, BF), "zt": _sb(4 * C, BF), "dd": _sb(4 * C, BF),
    "ut": _sb(512, BF), "vt": _sb(512, BF), "et": _sb(2048, BF), "ones": _sb(128, BF),
    "qu": _sb(128, Q4), "su": _sb(128, U8), "qu3": _sb(384, Q4), "su3": _sb(384, U8),
    "qv": _sb(128, Q4), "sv": _sb(128, U8), "qe": _sb(512, Q4), "se": _sb(512, U8),
    "qw": _sb(512, Q4), "sw": _sb(512, U8),
    "qj0": _sb(C, Q4), "sj0": _sb(C, U8), "qj1": _sb(C, Q4), "sj1": _sb(C, U8), "qj2": _sb(C, Q4), "sj2": _sb(C, U8),
    "qz": _sb(C, Q4), "sz": _sb(C, U8),
    "nbi": _sb(42, I32), "nb16": _sb(42, U16), "coli": _sb(4, I32), "colf": _sb(8, F32),
    "uli": _sb(24, I32), "ul16": _sb(24, U16),
    "r16": _sb(240, F32), "r4": _sb(C, F32), "jrow": _sb(C, F32), "jrow2": _sb(C, F32),
    "mask": _sb(C, F32), "chold": _sb(240, F32), "cd": _sb(C, BF), "c32": _sb(C, F32), "ctmp": _sb(C, F32), "cb": _sb(C, BF),
    "ct": _sb(42, F32), "jka": _sb(56, F32), "jkb": _sb(56, F32),
    "rm": _sb(240, F32), "hh": _sb(240, F32), "mv": _sb(7 * C, BF), "so": _sb(7 * 112, BF),
    "ta": _sb(10 * C, BF), "eq": _sb(C, BF), "dg": _sb(C, BF), "tr": _sb(42, F32), "trs": _sb(42, F32),
    "rk16": _sb(14, U16), "erow": _sb(C, F32), "es": _sb(K, F32),
    "ww": _sb(768, F32), "dn": _sb(4 * C, F32), "keep": _sb(C, F32), "nm": _sb(C, F32),
    "y0": _sb(C, F32), "y1": _sb(C, F32), "a0f": _sb(56, F32), "a1f": _sb(56, F32), "o0": _sb(56, U16), "o1": _sb(56, U16),
    "s0": _sb(C, F32), "b01": _sb(C, F32), "m1": _sb(C, BF), "m2": _sb(C, BF), "ym1": _sb(C, BF), "ym2": _sb(C, BF),
    "bt": _sb(56, F32), "b1": _sb(56, F32), "uu": _sb(56, F32), "vv": _sb(56, F32), "oz": _sb(56, U16), "ow": _sb(56, U16),
    "rr": _sb(4 * C, F32), "ysb": _sb(C, F32), "opr": _sb(C, F32),
}
for _t in range(R + 1):
    SCRATCH["qx%d" % _t] = _sb(C, Q4)
    SCRATCH["sx%d" % _t] = _sb(C, U8)
for _t in range(R):
    SCRATCH["lq%d" % _t] = _sb(C, Q4)
    SCRATCH["ls%d" % _t] = _sb(C, U8)
    SCRATCH["ll%d" % _t] = _sb(16, U16)
    SCRATCH["sl%d" % _t] = _sb(16, U16)
for _t in range(8):
    SCRATCH["ps%d" % _t] = ("psum", [128, 512], F32)

SEMAPHORES = ["cv", "ca", "cp", "cg", "sent"] + ["d%d" % i for i in range(20)] \
    + ["aq%d" % i for i in range(R)] + ["al%d" % i for i in range(R)]


def rank_program(g, core, T, topo):
    rank = T.rank_of(core)
    if rank is None:
        return
    A_, ACT = AluOpType, ActivationFunctionType
    nxt = T.cores[(rank + 1) % len(T.cores)]
    prv = T.cores[(rank - 1) % len(T.cores)]
    rid, pid, _se = topo.addr(nxt)
    emask, ne_out, ne_in = topo.mask(core, nxt), len(topo.engines(core, nxt)), len(topo.engines(prv, core))

    Q = {"V": g.vector, "A": g.scalar, "P": g.tensor, "S": g.sync, "G": g}
    own = {"V": "cv", "A": "ca", "P": "cp", "G": "cg"}
    clock = {k: {} for k in Q}
    count = {}
    wrote, readers = {}, {}
    ndma = [0]

    def wait(q, ev):
        sem, val, snap = ev[0], ev[1], ev[2]
        if clock[q].get(sem, 0) >= val:
            return
        Q[q].wait_ge(T.sem[sem], val)
        clock[q][sem] = val
        for s, v in snap.items():
            if clock[q].get(s, 0) < v:
                clock[q][s] = v

    def order(q, reads, writes):
        evs = []
        for k in reads:
            if k in wrote:
                evs.append(wrote[k])
            if k.startswith("ps"):
                evs += [e for e in readers.get(k, []) if e[3] != q]
        for k in writes:
            if k in wrote:
                evs.append(wrote[k])
            evs += readers.get(k, [])
        evs.sort(key=lambda e: -e[1])
        for e in evs:
            wait(q, e)

    def note(ev, reads, writes):
        for k in reads:
            readers.setdefault(k, []).append(ev)
        for k in writes:
            wrote[k] = ev
            readers[k] = []

    def op(q, reads, writes, call):
        order(q, reads, writes)
        sem = own[q]
        count[sem] = count.get(sem, 0) + 1
        call().then_inc(T.sem[sem], 1)
        note((sem, count[sem], dict(clock[q]), q), reads, writes)

    def dma(q, reads, writes, out, in_):
        order(q, reads, writes)
        sem = "d%d" % ndma[0]
        ndma[0] += 1
        count[sem] = 16
        Q[q].dma_start(out, in_).then_inc(T.sem[sem], 16)
        note((sem, 16, dict(clock[q]), "D"), reads, writes)

    def send(reads, out, in_, sem):
        order("G", reads, [])
        g.remote_dma(out, in_, T.sem[sem], T.sem.sent, pid, rid, emask)
        count["sent"] = count.get("sent", 0) + ne_out

    for t in range(R):
        wrote["lq%d" % t] = ("aq%d" % t, 2 * ne_in, {}, "R")
        wrote["ll%d" % t] = ("al%d" % t, ne_in, {}, "R")
        count["aq%d" % t], count["al%d" % t] = 2 * ne_in, ne_in

    V, S, PE = g.vector, g.scalar, g.tensor

    def ts(reads, writes, out, in0, s1, s2, op0, op1=None):
        if op1 is None:
            op("V", reads, writes, lambda: V.tensor_scalar(out, in0, s1, None, op0))
        else:
            op("V", reads, writes, lambda: V.tensor_scalar(out, in0, s1, s2, op0, op1))

    def tt(reads, writes, out, in0, in1, o):
        op("V", reads, writes, lambda: V.tensor_tensor(out, in0, in1, o))

    def scan(reads, writes, out, d0, d1, init, op0, op1):
        op("V", reads, writes, lambda: V.tensor_tensor_scan(out, d0, d1, init, op0, op1))

    def cp(reads, writes, out, in_):
        op("V", reads, writes, lambda: V.tensor_copy(out, in_))

    def ms(writes, ap, c):
        op("V", [], writes, lambda: V.memset(ap, c))

    def quant(reads, name, tile):
        op("V", reads, ["q" + name], lambda: V.quantize_mx(T["q" + name][:], T["s" + name][:], tile))

    def act(reads, writes, out, in_, func, **kw):
        op("A", reads, writes, lambda: S.activation(out, in_, func, **kw))

    def mm(bank, reads, wq, ws, xq, xs):
        op("P", reads, ["ps%d" % bank],
           lambda: PE.matmul_mx(T["ps%d" % bank][:, 0:C], wq, ws, xq, xs, True, True))

    def mmu(bank, r, name):
        mm(bank, ["qu3_%d" % r, "su3_%d" % r, "q" + name], T.qu3[:, 128 * r:128 * r + 128], T.su3[:, 128 * r:128 * r + 128],
           T["q" + name][:], T["s" + name][:])

    def iota(writes, out, pattern, base, cm, flt=True):
        if flt:
            op("G", [], writes, lambda: g.iota(out, pattern, base, cm, allow_small_or_imprecise_dtypes=True))
        else:
            op("G", [], writes, lambda: g.iota(out, pattern, base, cm))

    def ps(b):
        return T["ps%d" % b][:, 0:C]

    def col(i):
        return T.colf[:, i:i + 1]

    XK = ["X0", "X1", "X2", "X3"]
    J2K = ["J2_0", "J2_1", "J2_2", "J2_3"]
    DK = ["dd0", "dd1", "dd2", "dd3"]
    X = T.xs[:]

    def pick_codes(r):
        op("V", ["qu", "ul16"], ["qu3_%d" % r], lambda: V.tensor_copy(
            T.qu3[:, 128 * r:128 * r + 128].bitcast(dt.uint32), T.qu[:, 0:128].bitcast(dt.uint32).indirect(T.ul16[:, 8 * r:8 * r + 8])))

    def pick_scales(r):
        act(["qu", "ul16"], ["su3_%d" % r], T.su3[:, 128 * r:128 * r + 128], T.su[:, 0:128].indirect(T.ul16[:, 8 * r:8 * r + 8]), ACT.Copy)

    def n_minus_j(t, key, out):
        tt(["jrow", "jrow2", "nb16"], [key], out, T.jrow[:, 0:C].indirect(T.nb16[:, 14 * t:14 * t + 14]), T.jrow2[:], A_.subtract)

    def identity(b):
        op("G", ["ones", "et"], ["et%d" % b], lambda: g.affine_select(
            T.et[:, 512 * b + b:512 * b + 512:4], T.ones[:], [[-1, 128]], A_.is_equal, 0.0, 0, 1))

    dma("S", [], XK, X, T.x[:])
    dma("A", [], ["ut"], T.ut[:], T.u[:])
    dma("S", [], ["nbi"], T.nbi[:], T.nb[:])
    dma("S", [], ["XP"], T.pool[:, 0:4 * C], T.x[:])
    dma("S", [], ["J0"], T.jw[:, 0:4 * C], T.x[:])
    dma("S", [], ["vt"], T.vt[:], T.v[:])
    dma("S", [], ["qw"], T.qw[:].bitcast(dt.uint8), T.wc[:])
    dma("S", [], ["sw"], T.sw[:], T.ws[:])

    iota(["coli0"], T.coli[:, 0:1], [[0, 1]], 0, 1, False)
    iota(["uli"], T.uli[:], [[1, 3], [16, 8]], 0, 0, False)
    iota(["r4"], T.r4[:], [[0, 56], [1, 4]], 0, 0)
    iota(["r16"], T.r16[:], [[0, 15], [1, 16]], 0, 0)
    iota(["jrow"], T.jrow[:], [[1, C]], 0, 0)
    ms(["ones"], T.ones[:], 1.0)
    ms(["rmt"], T.rm[:, C:240], 0.0)
    ts(["coli0"], ["coli1"], T.coli[:, 1:2], T.coli[:, 0:1], 15, None, A_.bitwise_and)
    ts(["coli0"], ["coli2"], T.coli[:, 2:3], T.coli[:, 0:1], 15, 2, A_.bitwise_and, A_.logical_shift_right)
    ts(["coli0"], ["coli3"], T.coli[:, 3:4], T.coli[:, 0:1], 3, None, A_.bitwise_and)
    ms(["ct"], T.ct[:], 1.0)
    cp(["coli0", "coli1", "coli2", "coli3"], ["colf"], T.colf[:, 0:4], T.coli[:, 0:4])
    cp(["uli"], ["ul16"], T.ul16[:], T.uli[:])
    ms(["et"], T.et[:], 0.0)
    ms(["tr"], T.tr[:], 0.0)
    ts(["colf"], ["colk"], col(4), col(2), -1024.0, 3072.0, A_.mult, A_.add)
    ts(["colf"], ["colj"], col(7), col(2), -1023.0, 3072.0, A_.mult, A_.add)
    ms(["ct"], T.ct[:, 0:42:3], 0.0)
    ts(["r16", "colf"], ["mask"], T.mask[:], T.r16[:, 0:C], col(1), None, A_.is_equal)
    ts(["r16", "colf"], ["chold"], T.chold[:], T.r16[:], col(1), None, A_.not_equal)
    act(["r4", "colf"], ["ctmp"], T.ctmp[:], T.r4[:], ACT.Sign, bias=col(2), scale=-1.0)
    act(["ctmp"], ["ctmp"], T.ctmp[:], T.ctmp[:], ACT.Abs)
    act(["ctmp"], ["c32"], T.c32[:], T.ctmp[:], ACT.Identity, bias=16384.0, scale=-17408.0)
    for b in range(4):
        identity(b)
    quant(["ut"], "u", T.ut[:])
    quant(XK, "x0", X)
    pick_codes(0)
    pick_scales(0)
    act(["jrow"], ["jrow2"], T.jrow2[:], T.jrow[:], ACT.Copy)
    act(["jrow", "colj"], ["jka"], T.jka[:], T.jrow[:, 0:C:4], ACT.Identity, bias=col(7))
    ts(["mask"], ["cd"], T.cd[:], T.mask[:], 255.0, 1.0, A_.mult, A_.add)
    ts(["colk", "colf"], ["cole"], col(5), col(4), 4.0, col(3), A_.mult, A_.add)
    ms(["cd"], T.cd[:, 0:C:16], 0.0)

    for t in range(R):
        CV = CVS[t]
        CA = [c for c in range(14) if c not in CV]
        qx = "x%d" % t
        lq, ls, ll, sl = T["lq%d" % t], T["ls%d" % t], T["ll%d" % t], T["sl%d" % t]
        w0, w1 = T.ww[:, 0:C], T.ww[:, 256:256 + C]
        win = T.pool[:, 0:4 * C + 4 * K * t]
        GK = ["XP"] + ["G%d" % i for i in range(t)]
        send(["q" + qx], lq[:].bitcast(dt.uint8), T["q" + qx][:].bitcast(dt.uint8), "aq%d" % t)
        send(["q" + qx], ls[:], T["s" + qx][:], "aq%d" % t)
        iota(["W2"], T.ww[:, 512:768], [[-K, 4], [0, K]], C + K * t, 0)
        mmu(0, 0, qx)
        if t:
            mmu(2, 2, qx)
        mmu(1, 0, qx)

        tt(["ps0", "mask"], ["rm"], T.rm[:, 0:C], ps(0), T.mask[:], A_.mult)
        if t:
            ts(["ps2"], ["keep"], T.keep[:], ps(2), 0.0, None, A_.is_ge)
        else:
            cp(["nbi"], ["nb16"], T.nb16[:], T.nbi[:])
        scan(["chold", "rm", "rmt"], ["hh"], T.hh[:], T.chold[:], T.rm[:], 0.0, A_.mult, A_.add)
        if t:
            tt(["keep", "dn"], ["W0"], w0, T.keep[:], T.dn[:, 0:4 * C:4], A_.mult)
        else:
            n_minus_j(0, "W1", w1)

        for n, c in enumerate(CA):
            act(["ps1", "hh"], ["ta%d" % n, "tah%d" % n, "tal%d" % n], T.ta[:, C * n:C * n + C], ps(1), ACT.Sign,
                bias=T.hh[:, 16 * c + 15:16 * c + 16], scale=-1.0)
        for n, c in enumerate(CA):
            a = T.ta[:, C * n + 16 * c:C * n + C]
            act(["ta%d" % n, "tr"], ["tah%d" % n, "tr0_%d" % c], a, a, ACT.Sign, bias=-0.5, scale=-1.0, accum_out=T.tr[:, 3 * c:3 * c + 1])
            if c:
                a = T.ta[:, C * n:C * n + 16 * c]
                act(["ta%d" % n, "tr"], ["tal%d" % n, "tr1_%d" % c], a, a, ACT.Sign, bias=0.5, scale=-1.0, accum_out=T.tr[:, 3 * c + 1:3 * c + 2])

        def compare(n):
            c = CV[n]
            h = T.hh[:, 16 * c + 15:16 * c + 16]
            ts(["ps0", "hh"], ["mvl%d" % n], T.mv[:, C * n:C * n + 16 * c], T.ps0[:, 0:16 * c], h, 2.0, A_.is_ge, A_.mult)
            ts(["ps0", "hh"], ["mvh%d" % n], T.mv[:, C * n + 16 * c:C * n + C], T.ps0[:, 16 * c:C], h, 2.0, A_.is_gt, A_.mult)

        tt(["ps0", "hh"], ["eq"], T.eq[:], ps(0), T.hh[:, 16:240], A_.is_equal)
        compare(0)
        if t:
            scan(["c32", "W0"], ["y0"], T.y0[:], T.c32[:], w0, 0.0, A_.add, A_.min)
        scan(["cd", "eq"], ["dg"], T.dg[:], T.cd[:], T.eq[:], 0.0, A_.mult, A_.add)
        compare(1)
        if t:
            tt(["y0", "jka"], ["a0f"], T.a0f[:], T.y0[:, 3:C:4], T.jka[:], A_.add)
        ts(["dg", "tr"], ["tr2"], T.tr[:, 2:42:3], T.dg[:, 15:C:16], 1.0 / 128, None, A_.mult)
        compare(2)
        if t:
            ts(["a0f", "colf"], ["o0"], T.o0[:], T.a0f[:], 4.0, col(3), A_.mult, A_.add)
        for n in range(3, len(CV)):
            compare(n)
        if t:
            tt(["W0", "nb16", "nm"], ["W1"], w1, w0.indirect(T.nb16[:, 14 * t:14 * t + 14]), T.nm[:], A_.add)
        else:
            pick_codes(1)
        for n in range(len(CV)):
            scan(["mvl%d" % n, "mvh%d" % n], ["so%d" % n], T.so[:, 112 * n:112 * n + 112],
                 T.mv[:, C * n:C * n + 112], T.mv[:, C * n + 112:C * n + C], -float(C), A_.add, A_.add)
        if t:
            tt(XK + GK + ["o0"], ["J0"], T.jw[:, 0:4 * C], win.indirect(T.o0[:]), X, A_.max)
        else:
            quant(["et%d" % b for b in range(4)], "e", T.et[:])
        cp(["so%d" % n for n in range(len(CV))] + ["tr"], ["tr0_%d" % c for c in CV],
           T.tr[:, 3 * CV[0]:3 * CV[-1] + 1:3], T.so[:, 111:112 * len(CV):112])
        scan(["c32", "W1"], ["y1"], T.y1[:], T.c32[:], w1, 0.0, A_.add, A_.min)

        trk = ["tr0_%d" % c for c in range(14)] + ["tr1_%d" % c for c in CA if c] + ["tr2", "tr"]
        scan(trk + ["ct"], ["trs"], T.trs[:], T.ct[:], T.tr[:], 0.0, A_.mult, A_.add)
        tt(["y1", "jka"], ["a1f"], T.a1f[:], T.y1[:, 3:C:4], T.jka[:], A_.add)
        ts(["trs"], ["rk16"], T.rk16[:], T.trs[:, 2:42:3], 0.5, C / 2 + 0.25, A_.mult, A_.add)
        ts(["a1f", "colf"], ["o1"], T.o1[:], T.a1f[:], 4.0, col(3), A_.mult, A_.add)
        cp(["rk16", "jrow"], ["erow"], T.erow[:, 0:C].indirect(T.rk16[:]), T.jrow[:])
        if t:
            quant(["J0"], "j0", T.jw[:, 0:4 * C])
        else:
            ms(["jg0"], T.jw[:, 4 * C:1024], 0.0)
        scan(["c32", "erow"], ["es"], T.es[:], T.c32[:, 0:K], T.erow[:, 0:K], 0.0, A_.add, A_.min)
        if t == 0:
            ms(["jg1"], T.jw[:, 1024 + 4 * C:2048], 0.0)
        ts(["es", "cole"], ["sl%d" % t], sl[:], T.es[:, 3:K:4], 4.0, col(5), A_.mult, A_.add)
        send(["sl%d" % t], ll[:], sl[:], "al%d" % t)

        if t == 0:
            pick_scales(1)
        for b in range(4):
            mm(4 + b, ["qe", "lq%d" % t], T.qe[:, 128 * b:128 * b + 128], T.se[:, 128 * b:128 * b + 128], lq[:], ls[:])
        mmu(3, 1, "j0" if t else qx)
        for b in range(4):
            act(["ps%d" % (4 + b)], [DK[b]], T.dd[:, b:4 * C:4], ps(4 + b), ACT.Copy)
        act(["ps3"], ["s0"], T.s0[:], ps(3), ACT.Copy)
        if t == 0:
            act(["ctmp"], ["cb"], T.cb[:], T.ctmp[:], ACT.Identity, bias=32.0, scale=-34.0)
            act(["jka"], ["jkb"], T.jkb[:], T.jka[:], ACT.Copy, scale=1.0 / 512)
            pick_scales(2)

        tt(XK + GK + ["o1"], ["J1"], T.jw[:, 1024:1024 + 4 * C], win.indirect(T.o1[:]), X, A_.max)
        if t == 0:
            ms(["W0"], T.ww[:, 0:256], 0.0)
        quant(["J1"], "j1", T.jw[:, 1024:1024 + 4 * C])
        mmu(2, 1, "j1")
        if t == 0:
            ts(["colk"], ["colh"], col(6), col(4), -1.0 / 1024, None, A_.mult)
            ms(["Wg"], T.ww[:, 256 + C:512], 0.0)

        for i in range(4):
            w = min(4 * K, 4 * C - 4 * K * i)
            tt(XK + DK + ["ll%d" % t], [J2K[i]], T.jw[:, 2048 + 256 * i:2048 + 256 * i + w],
               T.dd[:, 0:4 * C].indirect(ll[:, 0:w // 16]), T.xs[:, 256 * i:256 * i + w], A_.max)
        if t + 1 < R:
            act(DK + ["ll%d" % t], ["G%d" % t], T.pool[:, 4 * C + 256 * t:4 * C + 256 * t + 256], T.dd[:, 0:4 * C].indirect(ll[:]), ACT.Copy)
        tt(["ps2", "s0"], ["m1"], T.m1[:], ps(2), T.s0[:], A_.is_gt)
        quant(J2K, "j2", T.jw[:, 2048:2048 + 4 * C])
        mmu(0, 1, "j2")

        tt(["ps2", "s0"], ["b01"], T.b01[:], ps(2), T.s0[:], A_.max)
        scan(["cb", "m1"], ["ym1"], T.ym1[:], T.cb[:], T.m1[:], 0.0, A_.add, A_.min)
        tt(["ps0", "b01"], ["m2"], T.m2[:], ps(0), T.b01[:], A_.is_gt)
        ts(["ym1", "colh"], ["bt"], T.bt[:], T.ym1[:, 3:C:4], 0.5, col(6), A_.mult, A_.add)
        scan(["cb", "m2"], ["ym2"], T.ym2[:], T.cb[:], T.m2[:], 0.0, A_.add, A_.min)
        tt(["bt", "jkb"], ["b1"], T.b1[:], T.bt[:], T.jkb[:], A_.add)
        tt(["ym2", "jkb"], ["uu"], T.uu[:], T.ym2[:, 3:C:4], T.jkb[:], A_.add)
        tt(["uu", "b1"], ["vv"], T.vv[:], T.uu[:], T.b1[:], A_.max)
        ts(["vv", "colf"], ["oz"], T.oz[:], T.vv[:], 2048.0, col(3), A_.mult, A_.add)
        ts(["vv"], ["ow"], T.ow[:], T.vv[:], 512.0, None, A_.mult)
        JK = ["J0", "J1", "jg0", "jg1", "oz"] + J2K
        jwin = T.jw[:, 0:2048 + 4 * C]
        act(JK, ["zb"], T.zt[:, 448:896], jwin.indirect(T.oz[:, 28:56]), ACT.Copy)
        cp(JK, ["za"], T.zt[:, 0:448], jwin.indirect(T.oz[:, 0:28]))
        quant(["za", "zb"], "z", T.zt[:])
        if t + 1 < R:
            n_minus_j(t + 1, "nm", T.nm[:])
        else:
            quant(["vt"], "v", T.vt[:])

        for b in range(4):
            mm(4 + b, ["qw", "sw", "qz"], T.qw[:, 128 * b:128 * b + 128], T.sw[:, 128 * b:128 * b + 128], T.qz[:], T.sz[:])
        for b in range(4):
            act(["ps%d" % (4 + b)], ["rr%d" % b], T.rr[:, C * b:C * b + C], ps(4 + b), ACT.Relu, scale=0.015625)
        act(["W0", "W1", "W2", "Wg", "ow"], ["dn"], T.dn[:], T.ww[:, 0:768].indirect(T.ow[:]), ACT.Copy)
        if t == 0:
            pick_codes(2)
        for b in range(4):
            xb = T.xs[:, b:4 * C:4]
            tt(["rr%d" % b, XK[b]], [XK[b]], xb, T.rr[:, C * b:C * b + C], xb, A_.add)
        quant(XK, "x%d" % (t + 1), X)
        if t + 1 < R:
            dma("S", XK, ["XP"], T.pool[:, 0:4 * C], X)

    qx = "x%d" % R
    mm(1, ["qv", "q" + qx], T.qv[:], T.sv[:], T["q" + qx][:], T["s" + qx][:])
    tt(["dn", "jrow"], ["opr"], T.opr[:], T.dn[:, 0:4 * C:4], T.jrow[:], A_.add)
    dma("S", ["q" + qx], [], T.oc[:], T["q" + qx][:].bitcast(dt.uint8))
    for k in range(4):
        dma("S", ["q" + qx], [], T.osc[4 * k:4 * k + 4, 0:C], T["s" + qx][32 * k:32 * k + 4, 0:C])
    act(["ps1"], ["ysb"], T.ysb[:], ps(1), ACT.Copy)
    dma("A", ["ysb"], [], T.y[:], T.ysb[:])
    dma("A", ["opr"], [], T.op[:], T.opr[0:128:16, 0:C])

    for sem, val in count.items():
        wait("G", (sem, val, {}, "E"))
